import numpy as np, ml_dtypes
CORES = [40,64,80,88,96,104,120,144]
N = 8
import mx_ref
NC = 128
CNT = [[0,0,8,36,0,44,0,40],[64,0,10,0,6,36,8,4],[0,6,0,8,68,0,20,26],[26,30,6,0,28,0,38,0],[8,34,30,12,0,6,26,12],[6,44,38,2,0,0,30,8],[12,6,24,6,0,42,0,38],[12,8,12,64,26,0,6,0]]
OFF = [[sum(c[:e]) for e in range(N + 1)] for c in CNT]
BF = ml_dtypes.bfloat16
def setup_inputs(rng):
    def f(*shape):
        return mx_ref.flush((rng.standard_normal(shape, dtype=np.float32) * np.exp2(rng.integers(-2, 3, shape[:-1] + (1,)))).astype(BF))
    return {"w": f(N, 128, 512), "x": f(N, 128, 4 * NC)}
def setup_inputs_blocks(rng):
    d = setup_inputs(rng)
    for k in ("w", "x"): d[k] = mx_ref.spread(d[k], rng, 4)
    return d
def setup_inputs_wide(rng):
    d = setup_inputs(rng)
    for k in ("w", "x"): d[k] = mx_ref.flush((d[k].astype(np.float32) * np.exp2(rng.integers(-8, 9, (N, 1, 1))).astype(np.float32)).astype(BF))
    return d
def setup_inputs_zeros(rng):
    d = setup_inputs(rng); v = d["x"].reshape(N, 128, -1, 4).copy()
    v[np.broadcast_to((rng.random((N, 1, v.shape[2], 1)) < 0.33), v.shape)] = 0
    d["x"] = v.reshape(d["x"].shape)
    return d
def reference(w, x):
    y = np.zeros((N, 128, NC), np.float32)
    for e in range(N):
        t = np.concatenate([x[j][:, 4 * OFF[j][e]:4 * OFF[j][e + 1]] for j in range(N)], axis=1)
        y[e] = mx_ref.matmul(mx_ref.quantize(w[e]), mx_ref.quantize(t))
    return {"y": y}

from concourse.bass import DstId, RemoteDMATransfer
from concourse.mybir import dt

HOSTS = 2
NC = 128

FEED_DIV = 1
OUT_DIV = 1
OWN_DIV = 1
PAD = False
STRAIGHT = 3

SCRATCH = {
    "xb": ("sbuf", [128, 4 * NC], "bfloat16"),
    "wb": ("sbuf", [128, 512], "bfloat16"),
    "xq": ("sbuf", [128, NC], "float8_e4m3fn_x4"),
    "xs": ("sbuf", [128, NC], "uint8"),
    "wq": ("sbuf", [128, 128], "float8_e4m3fn_x4"),
    "ws": ("sbuf", [128, 128], "uint8"),
    "bq": ("sbuf", [128, 512 if PAD else NC], "float8_e4m3fn_x4"),
    "bs": ("sbuf", [128, 512 if PAD else NC], "uint8"),
    "ps": ("psum", [128, 512], "float32"),
    "yb": ("sbuf", [128, NC], "float32"),
}
SEMAPHORES = ["ldx", "ldw", "qx", "qw", "got", "arr", "sent", "mm", "cp", "st"]

_CACHE = {}


def _bits(mask):
    return [b for b in range(mask.bit_length()) if (mask >> b) & 1]


def _mask(bits):
    m = 0
    for b in bits:
        m |= 1 << b
    return m


def _spread(bits, k):
    return bits[::len(bits) // k][:k]


def _plan(T, topo):
    if "plan" in _CACHE:
        return _CACHE["plan"]
    cores = [int(c) for c in T.cores]
    cnt = T.tables["CNT"]
    n = len(cores)
    world = range(HOSTS * topo.CORES_PER_HOST)
    off = [[sum(row[:e]) for e in range(n + 1)] for row in cnt]
    lots = []
    feed = {}
    inbound = {}
    for j, c in enumerate(cores):
        dests = [e for e in range(n) if e != j and cnt[j][e] > 0]
        own = sorted([e for e in dests if topo.may_write(c, cores[e])], key=lambda e: -cnt[j][e])
        far = [e for e in dests if not topo.may_write(c, cores[e])]
        chipmates = [k for k in world if k != c and topo.host(k) == topo.host(c) and topo.chip(k) == topo.chip(c)]
        ports = [k for k in chipmates if all(topo.may_write(k, cores[e]) for e in far)]
        dies = sorted({topo.die(k) for k in ports}, key=lambda d: d != topo.die(c))
        lanes = [[k for k in ports if topo.die(k) == d][:2] for d in dies]
        best = None
        for pick in range(len(lanes) ** len(far)):
            split = [[] for _ in lanes]
            p = pick
            for e in far:
                split[p % len(lanes)].append(e)
                p //= len(lanes)
            load = sum(sum(cnt[j][e] for e in s) ** 2 for s in split)
            for d, s in zip(dies, split):
                load += sum((inbound.get((e, d), 0) + cnt[j][e]) ** 2 - inbound.get((e, d), 0) ** 2 for e in s)
            key = (max(len(s) for s in split), load)
            if best is None or key < best[0]:
                best = (key, split)
        fd = {"codes": [], "scales": []}
        for d, lane, s in zip(dies, lanes, best[1] if best else []):
            if not s:
                continue
            s = sorted(s, key=lambda e: -cnt[j][e])
            for e in s:
                inbound[(e, d)] = inbound.get((e, d), 0) + cnt[j][e]
            lots.append((j, lane[0], lane[1], s, PAD))
            fd["codes"].append(lane[0])
            fd["scales"].append(lane[1])
        rest = own[STRAIGHT:]
        if rest:
            spare = sorted([k for k in chipmates if k not in ports], key=lambda k: topo.die(k) == topo.die(c))
            lots.append((j, spare[0], spare[-1], rest, PAD))
            fd["codes"].append(spare[0])
            fd["scales"].append(spare[-1])
        for e in own[:STRAIGHT]:
            lots.append((j, c, c, [e], False))
        feed[c] = fd
    wid = [[0] * n for _ in range(n)]
    win = [[0] * n for _ in range(n)]
    for j, _, _, s, fused in lots:
        for e in s:
            wid[j][e] = max(cnt[j][k] for k in s) if fused else cnt[j][e]
            win[j][e] = min(off[j][e], NC - wid[j][e])
    slot = [[sum(wid[i][e] for i in range(j)) for e in range(n)] for j in range(n)]
    calls = {}
    arr = [0] * n
    for j, cq, cs, s, fused in lots:
        own_core = cq == cores[j]
        groups = [s] if fused else [[e] for e in s]
        for grp in groups:
            for kind, sender in (("codes", cq), ("scales", cs)):
                share = 1
                while share < len(grp):
                    share *= 2
                call = []
                for i, e in enumerate(grp):
                    bits = _bits(topo.mask(sender, cores[e]))
                    bits = _spread(bits, len(bits) // (OWN_DIV if own_core else OUT_DIV))
                    k = len(bits) // share
                    call.append((kind, win[j][e], cores[e], slot[j][e], wid[j][e], bits[i * k:(i + 1) * k]))
                    arr[e] += k
                calls.setdefault(sender, []).append(call)
    take = []
    for e in range(n):
        runs = []
        y = 0
        for j in range(n):
            if cnt[j][e] == 0:
                continue
            p = slot[j][e] + off[j][e] - win[j][e]
            if runs and runs[-1][0] + runs[-1][2] == y and runs[-1][1] + runs[-1][2] == p:
                runs[-1][2] += cnt[j][e]
            else:
                runs.append([y, p, cnt[j][e]])
            y += cnt[j][e]
        take.append(runs)
    cols = [sum(wid[j][e] for j in range(n)) for e in range(n)]
    _CACHE["plan"] = {"feed": feed, "calls": calls, "arr": arr, "take": take, "cols": cols}
    return _CACHE["plan"]


def _view(codes, scales, kind, a, w):
    if kind == "codes":
        return codes[:, a:a + w].bitcast(dt.uint8)
    return scales[:, a:a + w]


def rank_program(g, core, T, topo):
    plan = _plan(T, topo)
    rank = T.rank_of(core)
    calls = plan["calls"].get(core, [])
    if rank is None and not calls:
        return
    sem = T.sem
    sent = 0
    if rank is not None:
        g.sync.dma_start(T.xb[:], T.x[:]).then_inc(sem.ldx, 16)
        g.scalar.wait_ge(sem.ldx, 16)
        g.scalar.dma_start(T.wb[:], T.w[:]).then_inc(sem.ldw, 16)
        g.vector.wait_ge(sem.ldx, 16)
        g.vector.quantize_mx(T.xq[:], T.xs[:], T.xb[:]).then_inc(sem.qx, 1)
        g.vector.wait_ge(sem.ldw, 16)
        g.vector.quantize_mx(T.wq[:], T.ws[:], T.wb[:]).then_inc(sem.qw, 1)
        g.wait_ge(sem.qx, 1)
        for kind in ("codes", "scales"):
            carriers = plan["feed"][core][kind]
            if not carriers:
                continue
            bits = None
            for k in carriers:
                b = _bits(topo.mask(core, k))
                bits = b if bits is None else [x for x in bits if x in b]
            bits = _spread(bits, len(bits) // FEED_DIV)
            ids = []
            for k in carriers:
                rid, pid = topo.addr(k, core)
                ids.append(DstId(rid=rid, pnc=pid))
            tile = _view(T.xq, T.xs, kind, 0, NC)
            g.remote_dma_fused([RemoteDMATransfer(dst_ids=ids, dma_engine_mask=_mask(bits), remote_sem=sem.got,
                                                  srcs=[tile], dsts=[tile for _ in carriers])], local_sem=sem.sent)
            sent += len(bits)
    else:
        src = [c for c in T.cores if topo.host(c) == topo.host(core) and topo.chip(c) == topo.chip(core)][0]
        bits = _bits(topo.mask(int(src), core))
        g.wait_ge(sem.got, len(bits) // FEED_DIV)
    for call in calls:
        if len(call) == 1:
            kind, a, dst, b, w, bits = call[0]
            rid, pid = topo.addr(dst, core)
            g.remote_dma(_view(T.bq, T.bs, kind, b, w), _view(T.xq, T.xs, kind, a, w), sem.arr, sem.sent, pid, rid, _mask(bits))
            sent += len(bits)
        else:
            trs = []
            for kind, a, dst, b, w, bits in call:
                rid, pid = topo.addr(dst, core)
                trs.append(RemoteDMATransfer(dst_ids=[DstId(rid=rid, pnc=pid)], dma_engine_mask=_mask(bits), remote_sem=sem.arr,
                                             src=_view(T.xq, T.xs, kind, a, w), dst=_view(T.bq, T.bs, kind, b, w)))
                sent += len(bits)
            g.remote_dma_fused(trs, local_sem=sem.sent)
    if rank is not None:
        n = plan["cols"][rank]
        g.tensor.wait_ge(sem.qw, 1)
        g.tensor.wait_ge(sem.arr, plan["arr"][rank])
        g.tensor.matmul_mx(T.ps[:, 0:n], T.wq[:], T.ws[:], T.bq[:, 0:n], T.bs[:, 0:n], True, True).then_inc(sem.mm, 1)
        g.vector.wait_ge(sem.mm, 1)
        take = plan["take"][rank]
        for y, p, w in take:
            g.vector.tensor_copy(T.yb[:, y:y + w], T.ps[:, p:p + w]).then_inc(sem.cp, 1)
        g.sync.wait_ge(sem.cp, len(take))
        g.sync.dma_start(T.y[:], T.yb[:]).then_inc(sem.st, 16)
        g.sync.wait_ge(sem.st, 16)
    g.wait_ge(sem.sent, sent)
